import numpy as np
import ml_dtypes


def mxq(x, axis, fmt="e4m3"):
    dtype, down = {"e4m3": (ml_dtypes.float8_e4m3fn, 7), "e5m2": (ml_dtypes.float8_e5m2, 14)}[fmt]
    v = np.moveaxis(np.asarray(x, np.float32).astype(ml_dtypes.bfloat16).astype(np.float64), axis, -1)
    blocks = v.reshape(v.shape[:-1] + (-1, 32))
    amax = np.abs(blocks).max(-1, keepdims=True)
    byte = np.maximum(np.where(amax > 0, np.frexp(amax)[1] - 1 + 127, 0) - down, 1)
    scale = np.exp2(byte - 127.0)
    codes = (blocks / scale).astype(np.float32).astype(dtype).astype(np.float64)
    return np.moveaxis((codes * scale).reshape(v.shape), -1, axis)


WIDE = False


def mx_kscale(k):
    if not WIDE:
        return np.ones(k)
    levels = np.array([10, -10, 5, -5, 0])
    if k % 512:
        return np.exp2(np.random.permutation(np.resize(levels, k // 32))).repeat(32)
    a = np.empty((k // 512, 16))
    for p in range(k // 512):
        a[p, :8] = np.random.permutation(np.resize(levels, 8))
        for g in range(8):
            far = levels[np.abs(levels - a[p, g]) >= 10]
            a[p, g + 8] = far[np.random.randint(len(far))]
    return np.exp2(a.ravel()).repeat(32)


def f64(x):
    return np.asarray(x).astype(np.float64)


def striped(idx):
    return np.tile(idx.reshape(-1, 16).T, (8, 1)).astype(np.uint16)


def unstriped(offs):
    return offs[:16].T.reshape(-1).astype(np.int64)


E2M1 = np.array([0.0, 0.5, 1.0, 1.5, 2.0, 3.0, 4.0, 6.0, -0.0, -0.5, -1.0, -1.5, -2.0, -3.0, -4.0, -6.0])


def pack_weight(w, fmt):
    k, n = w.shape
    w = f64(np.asarray(w, np.float32).astype(ml_dtypes.bfloat16)).reshape(k // 32, 32, n)
    amax = np.abs(w).max(1)
    if fmt == "e4m3":
        byte = np.frexp(amax)[1] - 1 + 127 - 7
    else:
        mant, ex = np.frexp(amax / 6.0)
        byte = np.where(mant > 0.5, ex, ex - 1) + 127
    byte = np.clip(np.where(amax > 0, byte, 1), 1, 254)
    scaled = (w * np.exp2(127.0 - byte)[:, None, :]).reshape(k, n).astype(np.float32)
    by_word = np.ascontiguousarray(scaled.reshape(k // 512, 128, 4, n).transpose(0, 1, 3, 2))
    if fmt == "e4m3":
        words = by_word.astype(ml_dtypes.float8_e4m3fn).view(np.uint8)
    else:
        c = by_word.astype(ml_dtypes.float4_e2m1fn).view(np.uint8) & 0xF
        words = (c[..., 0::2] | (c[..., 1::2] << 4)).reshape(k // 512, 128, 2 * n)
    return np.ascontiguousarray(words), np.ascontiguousarray(byte.astype(np.uint8).reshape(k // 512, 16, n))


def unpack_weight(words, scales, fmt):
    g, _, n = scales.shape
    words = np.ascontiguousarray(words).reshape(g, 128, n, -1)
    if fmt == "e4m3":
        vals = words.view(ml_dtypes.float8_e4m3fn).astype(np.float64)
    else:
        nib = np.empty((g, 128, n, 4), np.uint8)
        nib[..., 0::2] = words & 0xF
        nib[..., 1::2] = words >> 4
        vals = E2M1[nib]
    vals = vals * np.repeat(np.exp2(scales.astype(np.float64) - 127.0), 8, axis=1)[..., None]
    return vals.transpose(0, 1, 3, 2).reshape(g * 512, n)


def gelu(v):
    return 0.5 * v * (1.0 + np.tanh(np.sqrt(2.0 / np.pi) * (v + 0.044715 * v**3)))


def striped8(idx):
    return np.concatenate([v.reshape(-1, 16).T for v in idx]).astype(np.uint16)


def unstriped8(offs):
    return np.stack([offs[16 * g:16 * g + 16].T.reshape(-1) for g in range(8)]).astype(np.int64)


def heads(h, wgt, idx8):
    r = np.arange(h.shape[0])
    return wgt[r // 4 % 128] * h[r[:, None], idx8[r % 512 // 64]]


def put_heads(h, wgs, idx8, t2):
    r = np.arange(h.shape[0])
    page = np.zeros((h.shape[0], t2))
    page[r[:, None], idx8[r % 512 // 64]] = wgs[r // 4 % 128] * h
    return page


K, T, H, N, S, P, T2 = 512, 4096, 1024, 384, 1024, 1024, 2048

def setup_inputs():
    n = np.random.standard_normal
    s = mx_kscale(K)[:, None]
    u = mx_kscale(H)[:, None]
    d = {}
    d["tab_words"], d["tab_scales"] = pack_weight(n((K, T)) * s, "e4m3")
    d["offs"] = striped(np.random.permutation(T)[:S])
    d["w1"] = (n((K, H)) / K ** 0.5 / s * u.T).astype(np.float32)
    d["b1"] = (0.6 * n(H) * u[:, 0]).astype(np.float32)
    d["w2_words"], d["w2_scales"] = pack_weight(n((K, H)) / K ** 0.5 / s * u.T, "e2m1")
    d["wgs"] = np.repeat(np.random.uniform(0.5, 2.0, (8, S)), 16, axis=0).astype(np.float32)
    d["offs2"] = striped8(np.stack([np.random.permutation(T2)[:S] for _ in range(8)]))
    d["wgt"] = np.repeat(np.random.uniform(0.5, 2.0, (8, P)), 16, axis=0).astype(np.float32)
    d["offs3"] = striped8(np.stack([np.random.permutation(T2)[:P] for _ in range(8)]))
    d["lev"] = (n((H, P)) * u).astype(np.float32)
    d["w3"] = (n((H, N)) / H ** 0.5 / u).astype(np.float32)
    return d

def reference(tab_words, tab_scales, offs, w1, b1, w2_words, w2_scales, wgs, offs2, wgt, offs3, lev, w3):
    v = unpack_weight(tab_words, tab_scales, "e4m3")[:, unstriped(offs)]
    fill = (mxq(f64(w1), 0, "e4m3").T @ v) + f64(b1)[:, None]
    room = unpack_weight(w2_words, w2_scales, "e2m1").T @ v
    h = np.minimum(fill, room)
    page = put_heads(h, f64(wgs), unstriped8(offs2), T2)
    x = heads(page, f64(wgt), unstriped8(offs3))
    z = np.abs(x - f64(lev))
    out = mxq(f64(w3), 0, "e4m3").T @ mxq(z, 0, "e4m3")
    return out

@@ -1,0 +1,289 @@
+from contextlib import ExitStack
+
+import concourse.mybir as mybir
+from concourse.masks import make_identity
+
+K, T, H, N, S, M, T2 = 512, 4096, 1024, 384, 1024, 1024, 2048
+FLOPS = 2 * 2 * K * H * S + 2 * H * N * M
+
+F32 = mybir.dt.float32
+BF16 = mybir.dt.bfloat16
+I32 = mybir.dt.int32
+U32 = mybir.dt.uint32
+U16 = mybir.dt.uint16
+U8 = mybir.dt.uint8
+FP8X4 = mybir.dt.float8_e4m3fn_x4
+FP4X4 = mybir.dt.float4_e2m1fn_x4
+ALU = mybir.AluOpType
+ACT = mybir.ActivationFunctionType
+
+P = 128
+HALF = 512
+CHUNK = 256
+CHUNKS = M // CHUNK
+PLANES = 8
+
+
+def tile_list_lock_flight_adviser_kernel(
+    tc, tab_words, tab_scales, offs, w1, b1, w2_words, w2_scales, wgs, offs2, wgt, offs3, lev, w3, out
+):
+    nc = tc.nc
+    with ExitStack() as ctx:
+        lists = ctx.enter_context(tc.tile_pool(name="lists", bufs=1))
+        keep = ctx.enter_context(tc.tile_pool(name="keep", bufs=1))
+        ring = ctx.enter_context(tc.tile_pool(name="ring", bufs=2))
+        levs = ctx.enter_context(tc.tile_pool(name="levs", bufs=3))
+        psum = ctx.enter_context(tc.psum_pool(name="psum", bufs=1))
+        psum2 = ctx.enter_context(tc.psum_pool(name="psum2", bufs=2))
+
+        list1 = lists.tile([P, S // 16], U16, name="list1")
+        list2 = lists.tile([P, S // 16], U16, name="list2")
+        list3 = lists.tile([P, M // 16], U16, name="list3")
+
+        tab_plane = keep.tile([P, T], U8, name="tab_plane", align_bytes=64)
+        nc.vector.memset(tab_plane[:].bitcast(I32), 0)
+        w2_plane_raw = keep.tile([P, H], U8, name="w2_plane_raw", align_bytes=64)
+        nc.vector.memset(w2_plane_raw[:].bitcast(I32), 0)
+
+        nc.sync.dma_start(list1[:], offs)
+        for q in range(4):
+            nc.scalar.dma_start(
+                tab_plane[32 * q : 32 * q + 4, :].bitcast(I32), tab_scales[0, 4 * q : 4 * q + 4, :].bitcast(I32)
+            )
+        for q in range(4):
+            nc.gpsimd.dma_start(
+                w2_plane_raw[32 * q : 32 * q + 4, :].bitcast(I32), w2_scales[0, 4 * q : 4 * q + 4, :].bitcast(I32)
+            )
+        bias = keep.tile([P, 2, 4], F32, name="bias")
+        nc.gpsimd.dma_start(bias[:], b1.rearrange("(b p i) -> p b i", b=2, i=4))
+
+        w2_raw = keep.tile([P, 2 * H], U8, name="w2_raw", align_bytes=64)
+        nc.sync.dma_start(w2_raw[:].bitcast(I32), w2_words[0].bitcast(I32))
+
+        w1_rows = w1.rearrange("(p j) c -> p j c", j=4)
+        w1_codes, w1_planes = [], []
+
+        def load_w1(b):
+            raw = keep.tile([P, 4, HALF], F32, name="w1_raw%d" % b)
+            nc.sync.dma_start(raw[:], w1_rows[:, :, b * HALF : (b + 1) * HALF])
+            return raw
+
+        def quantise_w1(b, raw):
+            grouped = keep.tile([P, 4 * HALF], BF16, name="w1_grouped%d" % b, align_bytes=64)
+            nc.scalar.copy(
+                grouped[:].rearrange("p (i q j) -> p q i j", i=4, j=4),
+                raw[:].rearrange("p j (q i) -> p q i j", i=4),
+            )
+            codes = keep.tile([P, HALF], U32, name="w1_codes%d" % b, align_bytes=64)
+            plane = keep.tile([P, HALF], U8, name="w1_plane%d" % b, align_bytes=64)
+            nc.vector.quantize_mx(codes[:].bitcast(FP8X4), plane[:], grouped[:])
+            w1_codes.append(codes)
+            w1_planes.append(plane)
+
+        w1_raw0 = load_w1(0)
+        tab = keep.tile([P, T], I32, name="tab")
+        nc.sync.dma_start(tab[:], tab_words[0].rearrange("p t i -> p (t i)").bitcast(I32))
+        nc.sync.dma_start(list2[:], offs2)
+        put_weight = keep.tile([P, S], F32, name="put_weight")
+        nc.sync.dma_start(put_weight[:], wgs)
+        nc.sync.dma_start(list3[:], offs3)
+        read_weight = keep.tile([P, M], F32, name="read_weight")
+        nc.sync.dma_start(read_weight[:], wgt)
+
+        pages = []
+        for k in range(2):
+            page = keep.tile([P, T2], F32, name="page%d" % k)
+            nc.vector.memset(page[:], 0.0)
+            pages.append(page)
+        ident = keep.tile([P, P], F32, name="ident")
+        make_identity(nc, ident[:])
+
+        w2_codes = keep.tile([P, 2 * H], U8, name="w2_codes", align_bytes=64)
+        nc.vector.tensor_copy(
+            w2_codes[:].rearrange("p (b i q e) -> p b i q e", b=2, i=4, e=2),
+            w2_raw[:].rearrange("p (b q i e) -> p b i q e", b=2, i=4, e=2),
+        )
+        v_plane = keep.tile([P, S], U8, name="v_plane", align_bytes=64)
+        nc.vector.tensor_copy(v_plane[:], tab_plane[:].indirect(list1[:]))
+        w2_plane = keep.tile([P, H], U8, name="w2_plane", align_bytes=64)
+        nc.vector.tensor_copy(
+            w2_plane[:].rearrange("p (b i q) -> p b i q", b=2, i=4),
+            w2_plane_raw[:].rearrange("p (b q i) -> p b i q", b=2, i=4),
+        )
+        quantise_w1(0, w1_raw0)
+
+        v_codes = []
+        for a in range(2):
+            codes = keep.tile([P, HALF], U32, name="v_codes%d" % a, align_bytes=64)
+            nc.vector.tensor_copy(codes[:], tab[:].bitcast(U32).indirect(list1[:, 32 * a : 32 * a + 32]))
+            v_codes.append(codes)
+
+        minus_read_weight = keep.tile([P, M], F32, name="minus_read_weight")
+        nc.scalar.mul(minus_read_weight[:], read_weight[:], -1.0)
+
+        lev_rows = lev.rearrange("(b p i) m -> b i p m", b=2, i=4)
+
+        def load_lev(n):
+            rows = levs.tile([P, M], F32, name="lev_rows")
+            nc.sync.dma_start(rows[:], lev_rows[n // 4, n % 4])
+            return rows
+
+        w3_rows = w3.rearrange("(b p j) n -> b p j n", b=2, j=4)
+        w3_codes, w3_planes = [], []
+
+        def quantise_w3(b):
+            raw = keep.tile([P, 4, N], F32, name="w3_raw%d" % b)
+            nc.sync.dma_start(raw[:], w3_rows[b])
+            grouped = keep.tile([P, 4 * N], BF16, name="w3_grouped%d" % b, align_bytes=64)
+            nc.scalar.copy(
+                grouped[:].rearrange("p (c i j) -> p c j i", i=4, j=4),
+                raw[:].rearrange("p j (c i) -> p c j i", i=4),
+            )
+            codes = keep.tile([P, N], U32, name="w3_codes%d" % b, align_bytes=64)
+            plane = keep.tile([P, N], U8, name="w3_plane%d" % b, align_bytes=64)
+            nc.vector.quantize_mx(codes[:].bitcast(FP8X4), plane[:], grouped[:])
+            w3_codes.append(codes)
+            w3_planes.append(plane)
+
+        def tighter_score(n):
+            b, i = divmod(n, 4)
+            h = ring.tile([P, S], F32, name="h")
+            room = ring.tile([P, S], F32, name="room")
+            fills = []
+            for a in range(2):
+                cols = slice(a * HALF, (a + 1) * HALF)
+                room_ps = psum.tile([P, HALF], F32, name="room_ps", tag="room%d" % a)
+                nc.tensor.matmul_mx(
+                    room_ps[:],
+                    lhsT=w2_codes[:, 2 * P * n : 2 * P * (n + 1)].bitcast(FP4X4),
+                    lhsT_scale=w2_plane[:, P * n : P * (n + 1)],
+                    rhs=v_codes[a][:].bitcast(FP8X4),
+                    rhs_scale=v_plane[:, cols],
+                    start=True,
+                    stop=True,
+                )
+                fill_ps = psum.tile([P, HALF], F32, name="fill_ps", tag="fill%d" % a)
+                nc.tensor.matmul_mx(
+                    fill_ps[:],
+                    lhsT=w1_codes[b][:, P * i : P * (i + 1)].bitcast(FP8X4),
+                    lhsT_scale=w1_planes[b][:, P * i : P * (i + 1)],
+                    rhs=v_codes[a][:].bitcast(FP8X4),
+                    rhs_scale=v_plane[:, cols],
+                    start=True,
+                    stop=True,
+                )
+                nc.scalar.copy(room[:, cols], room_ps[:])
+                fills.append(fill_ps)
+            for a in range(2):
+                cols = slice(a * HALF, (a + 1) * HALF)
+                nc.vector.scalar_tensor_tensor(
+                    h[:, cols], fills[a][:], bias[:, b, i : i + 1], room[:, cols], ALU.add, ALU.min
+                )
+            return h
+
+        def put(n, h):
+            nc.vector.tensor_tensor(pages[n % 2][:].indirect(list2[:]), h[:], put_weight[:], ALU.mult)
+
+        def read(n, first, count):
+            minus_x = ring.tile([P, count], F32, name="minus_x", tag="minus_x%d" % count, bufs=2 if count == M else 8)
+            nc.vector.tensor_tensor(
+                minus_x[:],
+                pages[n % 2][:].indirect(list3[:, first // 16 : (first + count) // 16]),
+                minus_read_weight[:, first : first + count],
+                ALU.mult,
+            )
+            return minus_x
+
+        def difference(bank, lev_cols, x_cols):
+            for k in range(CHUNK // P):
+                cols = slice(k * P, (k + 1) * P)
+                nc.tensor.matmul(bank[:, cols], lev_cols[:, cols], ident[:], start=True, stop=False, is_transpose=True)
+                nc.tensor.matmul(bank[:, cols], x_cols[:, cols], ident[:], start=False, stop=True, is_transpose=True)
+
+        turned = [
+            [keep.tile([P, 2, 2, P], F32, name="turned%d_%d" % (b, c)) for c in range(CHUNKS)] for b in range(2)
+        ]
+
+        def distance(n, lev_n, minus_x):
+            b, i = divmod(n, 4)
+            for c in range(CHUNKS):
+                cols = slice(c * CHUNK, (c + 1) * CHUNK)
+                bank = psum2.tile([P, CHUNK], F32, name="diff", tag="diff")
+                difference(bank, lev_n[:, cols], minus_x[:, cols])
+                halves = turned[b][c][:].bitcast(BF16).rearrange("m k u (p e) -> m k u p e", e=2)
+                nc.scalar.activation(
+                    halves[:, :, i // 2, :, i % 2], bank[:].rearrange("m (k p) -> m k p", k=2), ACT.Abs
+                )
+
+        def turn_back(b, c, words):
+            bank = psum2.tile([P, 2, CHUNK], F32, name="back", tag="back")
+            for u in range(2):
+                for k in range(CHUNK // P):
+                    nc.tensor.transpose(bank[:, u, k * P : (k + 1) * P], turned[b][c][:, k, u, :], ident[:])
+            nc.scalar.copy(words.rearrange("p (m u) -> p m u", u=2), bank[:].rearrange("p u m -> p m u"))
+
+        out_rows = out.rearrange("(t p) m -> p t m", p=P)
+
+        h_next = tighter_score(0)
+        lev_tiles = [load_lev(0)]
+        w1_raw1 = load_w1(1)
+        lev_tiles.append(load_lev(1))
+        for n in range(PLANES - 2):
+            put(n, h_next)
+            h_next = tighter_score(n + 1)
+            minus_x = read(n, 0, M)
+            lev_tiles.append(load_lev(n + 2))
+            distance(n, lev_tiles[n], minus_x)
+            if n == 0:
+                quantise_w1(1, w1_raw1)
+            if n in (1, 2):
+                quantise_w3(n - 1)
+            if n == 3:
+                z0_words = keep.tile([P, 2 * M], F32, name="z0_words", align_bytes=64)
+                for c in range(CHUNKS):
+                    turn_back(0, c, z0_words[:, 2 * c * CHUNK : 2 * (c + 1) * CHUNK])
+            if n == 4:
+                z0_codes = keep.tile([P, M], U32, name="z0_codes", align_bytes=64)
+                z0_plane = keep.tile([P, M], U8, name="z0_plane", align_bytes=64)
+                nc.vector.quantize_mx(z0_codes[:].bitcast(FP8X4), z0_plane[:], z0_words[:].bitcast(BF16))
+
+        put(6, h_next)
+        h_next = tighter_score(7)
+        early = read(6, 0, CHUNK)
+        put(7, h_next)
+        reads = []
+        for c in range(CHUNKS):
+            x6 = early if c == 0 else read(6, c * CHUNK, CHUNK)
+            reads.append((x6, read(7, c * CHUNK, CHUNK)))
+        for c in range(CHUNKS):
+            cols = slice(c * CHUNK, (c + 1) * CHUNK)
+            bank = psum2.tile([P, 2, CHUNK], F32, name="diff_pair", tag="diff")
+            for e in range(2):
+                difference(bank[:, e, :], lev_tiles[6 + e][:, cols], reads[c][e][:])
+            halves = turned[1][c][:].bitcast(BF16).rearrange("m k u (p e) -> m k u p e", e=2)
+            nc.scalar.activation(halves[:, :, 1, :, :], bank[:].rearrange("m e (k p) -> m k p e", k=2), ACT.Abs)
+            z1_words = ring.tile([P, 2 * CHUNK], F32, name="z1_words", align_bytes=64)
+            turn_back(1, c, z1_words[:])
+            z1_codes = ring.tile([P, CHUNK], U32, name="z1_codes", align_bytes=64)
+            z1_plane = ring.tile([P, CHUNK], U8, name="z1_plane", align_bytes=64)
+            nc.vector.quantize_mx(z1_codes[:].bitcast(FP8X4), z1_plane[:], z1_words[:].bitcast(BF16))
+            tag = ("fill%d", "room%d")[c % 2]
+            acc_a = psum.tile([P, 2, CHUNK], F32, name="acc_a", tag=tag % 0)
+            acc_b = psum.tile([P, CHUNK], F32, name="acc_b", tag=tag % 1)
+            sums = [acc_a[:, 0, :], acc_a[:, 1, :], acc_b[:]]
+            moving = [(z0_codes[:, cols], z0_plane[:, cols]), (z1_codes[:], z1_plane[:])]
+            for t in range(N // P):
+                for b in range(2):
+                    nc.tensor.matmul_mx(
+                        sums[t],
+                        lhsT=w3_codes[b][:, t * P : (t + 1) * P].bitcast(FP8X4),
+                        lhsT_scale=w3_planes[b][:, t * P : (t + 1) * P],
+                        rhs=moving[b][0].bitcast(FP8X4),
+                        rhs_scale=moving[b][1],
+                        start=(b == 0),
+                        stop=(b == 1),
+                    )
+            result = ring.tile([P, 3, CHUNK], F32, name="result", bufs=4)
+            nc.vector.tensor_copy(result[:, 0:2, :], acc_a[:])
+            nc.scalar.copy(result[:, 2, :], acc_b[:])
+            nc.sync.dma_start(out_rows[:, :, cols], result[:])

@@ -21,6 +21,7 @@ P = 128
 HALF = 512
 CHUNK = 256
 CHUNKS = M // CHUNK
+TAIL = [(0, 256), (256, 256), (512, 256), (768, 128), (896, 128)]
 PLANES = 8
 
 
@@ -40,12 +41,18 @@ def tile_list_lock_flight_adviser_kernel(
         list2 = lists.tile([P, S // 16], U16, name="list2")
         list3 = lists.tile([P, M // 16], U16, name="list3")
 
-        tab_plane = keep.tile([P, T], U8, name="tab_plane", align_bytes=64)
+        tab_plane = levs.tile([P, T], U8, name="tab_plane", tag="stage", align_bytes=64)
         nc.vector.memset(tab_plane[:].bitcast(I32), 0)
-        w2_plane_raw = keep.tile([P, H], U8, name="w2_plane_raw", align_bytes=64)
-        nc.vector.memset(w2_plane_raw[:].bitcast(I32), 0)
+        w2_plane_raw = levs.tile([P, H], U8, name="w2_plane_raw", tag="stage", align_bytes=64)
+        nc.gpsimd.memset(w2_plane_raw[:].bitcast(I32), 0)
 
         nc.sync.dma_start(list1[:], offs)
+        nc.sync.dma_start(list2[:], offs2)
+        nc.sync.dma_start(list3[:], offs3)
+        bias = keep.tile([P, 2, 4], F32, name="bias")
+        nc.sync.dma_start(bias[:], b1.rearrange("(b p i) -> p b i", b=2, i=4))
+        w2_raw = keep.tile([P, 2 * H], U8, name="w2_raw", tag="put_weight", align_bytes=64)
+        nc.sync.dma_start(w2_raw[:].bitcast(I32), w2_words[0].bitcast(I32))
         for q in range(4):
             nc.scalar.dma_start(
                 tab_plane[32 * q : 32 * q + 4, :].bitcast(I32), tab_scales[0, 4 * q : 4 * q + 4, :].bitcast(I32)
@@ -54,22 +61,17 @@ def tile_list_lock_flight_adviser_kernel(
             nc.gpsimd.dma_start(
                 w2_plane_raw[32 * q : 32 * q + 4, :].bitcast(I32), w2_scales[0, 4 * q : 4 * q + 4, :].bitcast(I32)
             )
-        bias = keep.tile([P, 2, 4], F32, name="bias")
-        nc.gpsimd.dma_start(bias[:], b1.rearrange("(b p i) -> p b i", b=2, i=4))
-
-        w2_raw = keep.tile([P, 2 * H], U8, name="w2_raw", align_bytes=64)
-        nc.sync.dma_start(w2_raw[:].bitcast(I32), w2_words[0].bitcast(I32))
 
         w1_rows = w1.rearrange("(p j) c -> p j c", j=4)
         w1_codes, w1_planes = [], []
 
         def load_w1(b):
-            raw = keep.tile([P, 4, HALF], F32, name="w1_raw%d" % b)
+            raw = keep.tile([P, 4, HALF], F32, name="w1_raw", tag="raw")
             nc.sync.dma_start(raw[:], w1_rows[:, :, b * HALF : (b + 1) * HALF])
             return raw
 
         def quantise_w1(b, raw):
-            grouped = keep.tile([P, 4 * HALF], BF16, name="w1_grouped%d" % b, align_bytes=64)
+            grouped = levs.tile([P, 4 * HALF], BF16, name="w1_grouped", tag=("stage", "later")[b], align_bytes=64)
             nc.scalar.copy(
                 grouped[:].rearrange("p (i q j) -> p q i j", i=4, j=4),
                 raw[:].rearrange("p j (q i) -> p q i j", i=4),
@@ -81,14 +83,8 @@ def tile_list_lock_flight_adviser_kernel(
             w1_planes.append(plane)
 
         w1_raw0 = load_w1(0)
-        tab = keep.tile([P, T], I32, name="tab")
+        tab = keep.tile([P, T], I32, name="tab", tag="tab")
         nc.sync.dma_start(tab[:], tab_words[0].rearrange("p t i -> p (t i)").bitcast(I32))
-        nc.sync.dma_start(list2[:], offs2)
-        put_weight = keep.tile([P, S], F32, name="put_weight")
-        nc.sync.dma_start(put_weight[:], wgs)
-        nc.sync.dma_start(list3[:], offs3)
-        read_weight = keep.tile([P, M], F32, name="read_weight")
-        nc.sync.dma_start(read_weight[:], wgt)
 
         pages = []
         for k in range(2):
@@ -100,9 +96,11 @@ def tile_list_lock_flight_adviser_kernel(
 
         w2_codes = keep.tile([P, 2 * H], U8, name="w2_codes", align_bytes=64)
         nc.vector.tensor_copy(
-            w2_codes[:].rearrange("p (b i q e) -> p b i q e", b=2, i=4, e=2),
-            w2_raw[:].rearrange("p (b q i e) -> p b i q e", b=2, i=4, e=2),
+            w2_codes[:].bitcast(U16).rearrange("p (b i q) -> p b i q", b=2, i=4),
+            w2_raw[:].bitcast(U16).rearrange("p (b q i) -> p b i q", b=2, i=4),
         )
+        put_weight = keep.tile([P, S], F32, name="put_weight", tag="put_weight", align_bytes=64)
+        nc.sync.dma_start(put_weight[:], wgs)
         v_plane = keep.tile([P, S], U8, name="v_plane", align_bytes=64)
         nc.vector.tensor_copy(v_plane[:], tab_plane[:].indirect(list1[:]))
         w2_plane = keep.tile([P, H], U8, name="w2_plane", align_bytes=64)
@@ -118,13 +116,15 @@ def tile_list_lock_flight_adviser_kernel(
             nc.vector.tensor_copy(codes[:], tab[:].bitcast(U32).indirect(list1[:, 32 * a : 32 * a + 32]))
             v_codes.append(codes)
 
+        read_weight = keep.tile([P, M], F32, name="read_weight", tag="tab")
+        nc.sync.dma_start(read_weight[:], wgt)
         minus_read_weight = keep.tile([P, M], F32, name="minus_read_weight")
         nc.scalar.mul(minus_read_weight[:], read_weight[:], -1.0)
 
         lev_rows = lev.rearrange("(b p i) m -> b i p m", b=2, i=4)
 
         def load_lev(n):
-            rows = levs.tile([P, M], F32, name="lev_rows")
+            rows = levs.tile([P, M], F32, name="lev_rows", tag="stage", align_bytes=64)
             nc.sync.dma_start(rows[:], lev_rows[n // 4, n % 4])
             return rows
 
@@ -132,7 +132,7 @@ def tile_list_lock_flight_adviser_kernel(
         w3_codes, w3_planes = [], []
 
         def quantise_w3(b):
-            raw = keep.tile([P, 4, N], F32, name="w3_raw%d" % b)
+            raw = keep.tile([P, 4, N], F32, name="w3_raw", tag="raw")
             nc.sync.dma_start(raw[:], w3_rows[b])
             grouped = keep.tile([P, 4 * N], BF16, name="w3_grouped%d" % b, align_bytes=64)
             nc.scalar.copy(
@@ -179,10 +179,18 @@ def tile_list_lock_flight_adviser_kernel(
                 nc.vector.scalar_tensor_tensor(
                     h[:, cols], fills[a][:], bias[:, b, i : i + 1], room[:, cols], ALU.add, ALU.min
                 )
+                if n == 0:
+                    put(n, h, a * HALF, HALF)
             return h
 
-        def put(n, h):
-            nc.vector.tensor_tensor(pages[n % 2][:].indirect(list2[:]), h[:], put_weight[:], ALU.mult)
+        def put(n, h, first, count):
+            cols = slice(first, first + count)
+            nc.vector.tensor_tensor(
+                pages[n % 2][:].indirect(list2[:, first // 16 : (first + count) // 16]),
+                h[:, cols],
+                put_weight[:, cols],
+                ALU.mult,
+            )
 
         def read(n, first, count):
             minus_x = ring.tile([P, count], F32, name="minus_x", tag="minus_x%d" % count, bufs=2 if count == M else 8)
@@ -194,33 +202,46 @@ def tile_list_lock_flight_adviser_kernel(
             )
             return minus_x
 
-        def difference(bank, lev_cols, x_cols):
-            for k in range(CHUNK // P):
-                cols = slice(k * P, (k + 1) * P)
-                nc.tensor.matmul(bank[:, cols], lev_cols[:, cols], ident[:], start=True, stop=False, is_transpose=True)
-                nc.tensor.matmul(bank[:, cols], x_cols[:, cols], ident[:], start=False, stop=True, is_transpose=True)
-
+        spans = [[(first, CHUNK) for first in range(0, M, CHUNK)], TAIL]
         turned = [
-            [keep.tile([P, 2, 2, P], F32, name="turned%d_%d" % (b, c)) for c in range(CHUNKS)] for b in range(2)
+            [
+                [keep.tile([P, count // P, P], F32, name="turned%d_%d_%d" % (b, c, u)) for u in range(2)]
+                for c, (first, count) in enumerate(spans[b])
+            ]
+            for b in range(2)
         ]
 
-        def distance(n, lev_n, minus_x):
-            b, i = divmod(n, 4)
-            for c in range(CHUNKS):
-                cols = slice(c * CHUNK, (c + 1) * CHUNK)
-                bank = psum2.tile([P, CHUNK], F32, name="diff", tag="diff")
-                difference(bank, lev_n[:, cols], minus_x[:, cols])
-                halves = turned[b][c][:].bitcast(BF16).rearrange("m k u (p e) -> m k u p e", e=2)
-                nc.scalar.activation(
-                    halves[:, :, i // 2, :, i % 2], bank[:].rearrange("m (k p) -> m k p", k=2), ACT.Abs
+        def turn(bank, rows, start, stop):
+            blocks = rows.shape[1] // P
+            for k in range(blocks):
+                nc.tensor.matmul(
+                    bank[:, k * P : (k + 1) * P],
+                    rows[:, k * P : (k + 1) * P],
+                    ident[:],
+                    start=start and k == 0,
+                    stop=stop and k == blocks - 1,
+                    is_transpose=True,
                 )
 
-        def turn_back(b, c, words):
-            bank = psum2.tile([P, 2, CHUNK], F32, name="back", tag="back")
+        def absolute(n, c, bank):
+            b, i = divmod(n, 4)
+            halves = turned[b][c][i // 2][:].bitcast(BF16).rearrange("m k (p e) -> m k p e", e=2)
+            nc.scalar.activation(halves[:, :, :, i % 2], bank[:].rearrange("m (k p) -> m k p", p=P), ACT.Abs)
+
+        def distance(n, lev_n, minus_x):
+            for c, (first, count) in enumerate(spans[n // 4]):
+                bank = psum2.tile([P, count], F32, name="diff", tag="diff")
+                turn(bank, lev_n[:, first : first + count], True, False)
+                turn(bank, minus_x[:, first : first + count], False, True)
+                absolute(n, c, bank)
+
+        def turn_back(b, c, words, copy):
+            count = spans[b][c][1]
+            bank = psum2.tile([P, 2, count], F32, name="back", tag="back")
             for u in range(2):
-                for k in range(CHUNK // P):
-                    nc.tensor.transpose(bank[:, u, k * P : (k + 1) * P], turned[b][c][:, k, u, :], ident[:])
-            nc.scalar.copy(words.rearrange("p (m u) -> p m u", u=2), bank[:].rearrange("p u m -> p m u"))
+                for k in range(count // P):
+                    nc.tensor.transpose(bank[:, u, k * P : (k + 1) * P], turned[b][c][u][:, k, :], ident[:])
+            copy(words.rearrange("p (m u) -> p m u", u=2), bank[:].rearrange("p u m -> p m u"))
 
         out_rows = out.rearrange("(t p) m -> p t m", p=P)
 
@@ -228,11 +249,13 @@ def tile_list_lock_flight_adviser_kernel(
         lev_tiles = [load_lev(0)]
         w1_raw1 = load_w1(1)
         lev_tiles.append(load_lev(1))
-        for n in range(PLANES - 2):
-            put(n, h_next)
+        for n in range(PLANES - 1):
+            if n > 0:
+                put(n, h_next, 0, S)
             h_next = tighter_score(n + 1)
             minus_x = read(n, 0, M)
-            lev_tiles.append(load_lev(n + 2))
+            if n + 2 < PLANES:
+                lev_tiles.append(load_lev(n + 2))
             distance(n, lev_tiles[n], minus_x)
             if n == 0:
                 quantise_w1(1, w1_raw1)
@@ -241,49 +264,87 @@ def tile_list_lock_flight_adviser_kernel(
             if n == 3:
                 z0_words = keep.tile([P, 2 * M], F32, name="z0_words", align_bytes=64)
                 for c in range(CHUNKS):
-                    turn_back(0, c, z0_words[:, 2 * c * CHUNK : 2 * (c + 1) * CHUNK])
+                    turn_back(0, c, z0_words[:, 2 * c * CHUNK : 2 * (c + 1) * CHUNK], nc.scalar.copy)
             if n == 4:
                 z0_codes = keep.tile([P, M], U32, name="z0_codes", align_bytes=64)
                 z0_plane = keep.tile([P, M], U8, name="z0_plane", align_bytes=64)
                 nc.vector.quantize_mx(z0_codes[:].bitcast(FP8X4), z0_plane[:], z0_words[:].bitcast(BF16))
 
-        put(6, h_next)
-        h_next = tighter_score(7)
-        early = read(6, 0, CHUNK)
-        put(7, h_next)
-        reads = []
-        for c in range(CHUNKS):
-            x6 = early if c == 0 else read(6, c * CHUNK, CHUNK)
-            reads.append((x6, read(7, c * CHUNK, CHUNK)))
-        for c in range(CHUNKS):
-            cols = slice(c * CHUNK, (c + 1) * CHUNK)
-            bank = psum2.tile([P, 2, CHUNK], F32, name="diff_pair", tag="diff")
-            for e in range(2):
-                difference(bank[:, e, :], lev_tiles[6 + e][:, cols], reads[c][e][:])
-            halves = turned[1][c][:].bitcast(BF16).rearrange("m k u (p e) -> m k u p e", e=2)
-            nc.scalar.activation(halves[:, :, 1, :, :], bank[:].rearrange("m e (k p) -> m k p e", k=2), ACT.Abs)
-            z1_words = ring.tile([P, 2 * CHUNK], F32, name="z1_words", align_bytes=64)
-            turn_back(1, c, z1_words[:])
-            z1_codes = ring.tile([P, CHUNK], U32, name="z1_codes", align_bytes=64)
-            z1_plane = ring.tile([P, CHUNK], U8, name="z1_plane", align_bytes=64)
-            nc.vector.quantize_mx(z1_codes[:].bitcast(FP8X4), z1_plane[:], z1_words[:].bitcast(BF16))
-            tag = ("fill%d", "room%d")[c % 2]
-            acc_a = psum.tile([P, 2, CHUNK], F32, name="acc_a", tag=tag % 0)
-            acc_b = psum.tile([P, CHUNK], F32, name="acc_b", tag=tag % 1)
-            sums = [acc_a[:, 0, :], acc_a[:, 1, :], acc_b[:]]
-            moving = [(z0_codes[:, cols], z0_plane[:, cols]), (z1_codes[:], z1_plane[:])]
+        last = PLANES - 1
+        put(last, h_next, 0, S)
+        reads = [read(last, first, count) for first, count in TAIL]
+
+        def open_difference(c, tag):
+            first, count = TAIL[c]
+            bank = psum.tile([P, count], F32, name="diff_last", tag=tag)
+            turn(bank, lev_tiles[last][:, first : first + count], True, False)
+            return bank
+
+        def close_difference(c, bank):
+            turn(bank, reads[c][:], False, True)
+            absolute(last, c, bank)
+
+        def multiply(c, b, accs, codes, plane):
+            per_bank = accs[0].shape[1]
             for t in range(N // P):
-                for b in range(2):
-                    nc.tensor.matmul_mx(
-                        sums[t],
-                        lhsT=w3_codes[b][:, t * P : (t + 1) * P].bitcast(FP8X4),
-                        lhsT_scale=w3_planes[b][:, t * P : (t + 1) * P],
-                        rhs=moving[b][0].bitcast(FP8X4),
-                        rhs_scale=moving[b][1],
-                        start=(b == 0),
-                        stop=(b == 1),
-                    )
-            result = ring.tile([P, 3, CHUNK], F32, name="result", bufs=4)
-            nc.vector.tensor_copy(result[:, 0:2, :], acc_a[:])
-            nc.scalar.copy(result[:, 2, :], acc_b[:])
-            nc.sync.dma_start(out_rows[:, :, cols], result[:])
+                place = t % per_bank
+                width = accs[t // per_bank].shape[1]
+                nc.tensor.matmul_mx(
+                    accs[t // per_bank][:, place, :],
+                    lhsT=w3_codes[b][:, t * P : (t + 1) * P].bitcast(FP8X4),
+                    lhsT_scale=w3_planes[b][:, t * P : (t + 1) * P],
+                    rhs=codes.bitcast(FP8X4),
+                    rhs_scale=plane,
+                    start=(b == 0 and place == 0),
+                    stop=(b == 1 and place == width - 1),
+                )
+
+        def open_sums(c, pool, tags):
+            first, count = TAIL[c]
+            widths = [2, 1] if len(tags) == 2 else [3]
+            accs = [pool.tile([P, w, count], F32, name="acc", tag=tag) for w, tag in zip(widths, tags)]
+            multiply(c, 0, accs, z0_codes[:, first : first + count], z0_plane[:, first : first + count])
+            return accs
+
+        def quantise_last(c, copy):
+            count = TAIL[c][1]
+            z1_words = ring.tile([P, 2 * count], F32, name="z1_words", align_bytes=64, bufs=5)
+            turn_back(1, c, z1_words[:], copy)
+            z1_codes = ring.tile([P, count], U32, name="z1_codes", align_bytes=64, bufs=5)
+            z1_plane = ring.tile([P, count], U8, name="z1_plane", align_bytes=64, bufs=5)
+            nc.vector.quantize_mx(z1_codes[:].bitcast(FP8X4), z1_plane[:], z1_words[:].bitcast(BF16))
+            return z1_codes, z1_plane
+
+        def close_sums(c, accs, z1, copies):
+            first, count = TAIL[c]
+            multiply(c, 1, accs, z1[0][:], z1[1][:])
+            result = ring.tile([P, N // P, count], F32, name="result", bufs=5)
+            t = 0
+            for acc, copy in zip(accs, copies):
+                copy(result[:, t : t + acc.shape[1], :], acc[:])
+                t = t + acc.shape[1]
+            nc.sync.dma_start(out_rows[:, :, first : first + count], result[:])
+
+        act, dve = nc.scalar.copy, nc.vector.tensor_copy
+        banks = [open_difference(c, tag) for c, tag in enumerate(["fill0", "fill1", "room0", "room1"])]
+        acc0 = open_sums(0, psum2, ["diff", "diff"])
+        close_difference(0, banks[0])
+        banks.append(open_difference(4, "fill0"))
+        close_difference(1, banks[1])
+        z0 = quantise_last(0, act)
+        close_difference(2, banks[2])
+        acc1 = open_sums(1, psum, ["fill1", "room0"])
+        z1 = quantise_last(1, act)
+        close_difference(3, banks[3])
+        close_difference(4, banks[4])
+        close_sums(0, acc0, z0, [act, dve])
+        acc2 = open_sums(2, psum, ["room1", "fill0"])
+        z2 = quantise_last(2, dve)
+        close_sums(1, acc1, z1, [dve, act])
+        z3 = quantise_last(3, act)
+        acc3 = open_sums(3, psum2, ["diff"])
+        close_sums(2, acc2, z2, [dve, act])
+        z4 = quantise_last(4, dve)
+        acc4 = open_sums(4, psum2, ["diff"])
+        close_sums(3, acc3, z3, [act])
+        close_sums(4, acc4, z4, [dve])

@@ -93,6 +93,8 @@ def tile_list_lock_flight_adviser_kernel(
             pages.append(page)
         ident = keep.tile([P, P], F32, name="ident")
         make_identity(nc, ident[:])
+        ident_bf16 = keep.tile([P, P], BF16, name="ident_bf16")
+        make_identity(nc, ident_bf16[:])
 
         w2_codes = keep.tile([P, 2 * H], U8, name="w2_codes", align_bytes=64)
         nc.vector.tensor_copy(
@@ -202,14 +204,21 @@ def tile_list_lock_flight_adviser_kernel(
             )
             return minus_x
 
-        spans = [[(first, CHUNK) for first in range(0, M, CHUNK)], TAIL]
-        turned = [
+        spans = [[(0, HALF), (HALF, HALF)], TAIL]
+        z_rows = [
+            [keep.tile([P, 4 * M], BF16, name="z_rows0", align_bytes=64)],
             [
-                [keep.tile([P, count // P, P], F32, name="turned%d_%d_%d" % (b, c, u)) for u in range(2)]
-                for c, (first, count) in enumerate(spans[b])
-            ]
-            for b in range(2)
+                keep.tile([P, 4 * count], BF16, name="z_rows1_%d" % c, align_bytes=64)
+                for c, (first, count) in enumerate(TAIL)
+            ],
         ]
+
+        def z_slot(n, c):
+            b, i = divmod(n, 4)
+            first, count = spans[b][c]
+            if b == 0:
+                return z_rows[0][0][:].rearrange("p (m i) -> p m i", i=4)[:, first : first + count, i]
+            return z_rows[1][c][:].rearrange("p (m i) -> p m i", i=4)[:, :, i]
 
         def turn(bank, rows, start, stop):
             blocks = rows.shape[1] // P
@@ -223,25 +232,27 @@ def tile_list_lock_flight_adviser_kernel(
                     is_transpose=True,
                 )
 
-        def absolute(n, c, bank):
-            b, i = divmod(n, 4)
-            halves = turned[b][c][i // 2][:].bitcast(BF16).rearrange("m k (p e) -> m k p e", e=2)
-            nc.scalar.activation(halves[:, :, :, i % 2], bank[:].rearrange("m (k p) -> m k p", p=P), ACT.Abs)
-
         def distance(n, lev_n, minus_x):
-            for c, (first, count) in enumerate(spans[n // 4]):
-                bank = psum2.tile([P, count], F32, name="diff", tag="diff")
-                turn(bank, lev_n[:, first : first + count], True, False)
-                turn(bank, minus_x[:, first : first + count], False, True)
-                absolute(n, c, bank)
+            for a in range(2):
+                cols = slice(a * HALF, (a + 1) * HALF)
+                bank = psum2.tile([P, HALF], F32, name="diff", tag="diff")
+                turn(bank, lev_n[:, cols], True, False)
+                turn(bank, minus_x[:, cols], False, True)
+                turned = ring.tile([P, HALF], BF16, name="turned")
+                nc.scalar.activation(turned[:], bank[:], ACT.Abs)
+                back = psum2.tile([P, HALF], BF16, name="back", tag="back")
+                for k in range(HALF // P):
+                    block = slice(k * P, (k + 1) * P)
+                    nc.tensor.transpose(back[:, block], turned[:, block], ident_bf16[:])
+                for c, (first, count) in enumerate(spans[n // 4]):
+                    if first // HALF == a:
+                        nc.scalar.copy(z_slot(n, c), back[:, first - a * HALF : first - a * HALF + count])
 
-        def turn_back(b, c, words, copy):
-            count = spans[b][c][1]
-            bank = psum2.tile([P, 2, count], F32, name="back", tag="back")
-            for u in range(2):
-                for k in range(count // P):
-                    nc.tensor.transpose(bank[:, u, k * P : (k + 1) * P], turned[b][c][u][:, k, :], ident[:])
-            copy(words.rearrange("p (m u) -> p m u", u=2), bank[:].rearrange("p u m -> p m u"))
+        def quantise_z(rows, count, label):
+            codes = keep.tile([P, count], U32, name="z_codes" + label, align_bytes=64)
+            plane = keep.tile([P, count], U8, name="z_plane" + label, align_bytes=64)
+            nc.vector.quantize_mx(codes[:].bitcast(FP8X4), plane[:], rows[:])
+            return codes, plane
 
         out_rows = out.rearrange("(t p) m -> p t m", p=P)
 
@@ -261,28 +272,17 @@ def tile_list_lock_flight_adviser_kernel(
                 quantise_w1(1, w1_raw1)
             if n in (1, 2):
                 quantise_w3(n - 1)
-            if n == 3:
-                z0_words = keep.tile([P, 2 * M], F32, name="z0_words", align_bytes=64)
-                for c in range(CHUNKS):
-                    turn_back(0, c, z0_words[:, 2 * c * CHUNK : 2 * (c + 1) * CHUNK], nc.scalar.copy)
-            if n == 4:
-                z0_codes = keep.tile([P, M], U32, name="z0_codes", align_bytes=64)
-                z0_plane = keep.tile([P, M], U8, name="z0_plane", align_bytes=64)
-                nc.vector.quantize_mx(z0_codes[:].bitcast(FP8X4), z0_plane[:], z0_words[:].bitcast(BF16))
+            if n == 5:
+                z0_codes, z0_plane = quantise_z(z_rows[0][0], M, "0")
 
         last = PLANES - 1
         put(last, h_next, 0, S)
-        reads = [read(last, first, count) for first, count in TAIL]
 
-        def open_difference(c, tag):
+        def distance_last(c, minus_x):
             first, count = TAIL[c]
-            bank = psum.tile([P, count], F32, name="diff_last", tag=tag)
-            turn(bank, lev_tiles[last][:, first : first + count], True, False)
-            return bank
-
-        def close_difference(c, bank):
-            turn(bank, reads[c][:], False, True)
-            absolute(last, c, bank)
+            difference = keep.tile([P, count], F32, name="difference_last%d" % c)
+            nc.vector.tensor_tensor(difference[:], minus_x[:], lev_tiles[last][:, first : first + count], ALU.add)
+            nc.scalar.activation(z_slot(last, c), difference[:], ACT.Abs)
 
         def multiply(c, b, accs, codes, plane):
             per_bank = accs[0].shape[1]
@@ -306,15 +306,6 @@ def tile_list_lock_flight_adviser_kernel(
             multiply(c, 0, accs, z0_codes[:, first : first + count], z0_plane[:, first : first + count])
             return accs
 
-        def quantise_last(c, copy):
-            count = TAIL[c][1]
-            z1_words = ring.tile([P, 2 * count], F32, name="z1_words", align_bytes=64, bufs=5)
-            turn_back(1, c, z1_words[:], copy)
-            z1_codes = ring.tile([P, count], U32, name="z1_codes", align_bytes=64, bufs=5)
-            z1_plane = ring.tile([P, count], U8, name="z1_plane", align_bytes=64, bufs=5)
-            nc.vector.quantize_mx(z1_codes[:].bitcast(FP8X4), z1_plane[:], z1_words[:].bitcast(BF16))
-            return z1_codes, z1_plane
-
         def close_sums(c, accs, z1, copies):
             first, count = TAIL[c]
             multiply(c, 1, accs, z1[0][:], z1[1][:])
@@ -326,25 +317,24 @@ def tile_list_lock_flight_adviser_kernel(
             nc.sync.dma_start(out_rows[:, :, first : first + count], result[:])
 
         act, dve = nc.scalar.copy, nc.vector.tensor_copy
-        banks = [open_difference(c, tag) for c, tag in enumerate(["fill0", "fill1", "room0", "room1"])]
-        acc0 = open_sums(0, psum2, ["diff", "diff"])
-        close_difference(0, banks[0])
-        banks.append(open_difference(4, "fill0"))
-        close_difference(1, banks[1])
-        z0 = quantise_last(0, act)
-        close_difference(2, banks[2])
-        acc1 = open_sums(1, psum, ["fill1", "room0"])
-        z1 = quantise_last(1, act)
-        close_difference(3, banks[3])
-        close_difference(4, banks[4])
-        close_sums(0, acc0, z0, [act, dve])
-        acc2 = open_sums(2, psum, ["room1", "fill0"])
-        z2 = quantise_last(2, dve)
-        close_sums(1, acc1, z1, [dve, act])
-        z3 = quantise_last(3, act)
-        acc3 = open_sums(3, psum2, ["diff"])
-        close_sums(2, acc2, z2, [dve, act])
-        z4 = quantise_last(4, dve)
-        acc4 = open_sums(4, psum2, ["diff"])
-        close_sums(3, acc3, z3, [act])
-        close_sums(4, acc4, z4, [dve])
+        places = [
+            (psum, ["fill0", "fill1"]),
+            (psum, ["room0", "room1"]),
+            (psum2, ["diff", "diff"]),
+            (psum2, ["back"]),
+            (psum2, ["back"]),
+        ]
+        copies = [[dve, dve], [act, dve], [act, dve], [act], [dve]]
+        accs = [open_sums(c, *places[c]) for c in range(len(TAIL))]
+        xs = [read(last, *TAIL[0])]
+        zs = []
+        for c in range(len(TAIL)):
+            if c + 1 < len(TAIL):
+                xs.append(read(last, *TAIL[c + 1]))
+            distance_last(c, xs[c])
+            if c >= 2:
+                zs.append(quantise_z(z_rows[1][c - 2], TAIL[c - 2][1], "1_%d" % (c - 2)))
+        for c in range(len(TAIL)):
+            if c + 3 < len(TAIL):
+                zs.append(quantise_z(z_rows[1][c + 3], TAIL[c + 3][1], "1_%d" % (c + 3)))
+            close_sums(c, accs[c], zs[c], copies[c])

from contextlib import ExitStack

import concourse.mybir as mybir
from concourse.masks import make_identity

K, T, H, N, S, M, T2 = 512, 4096, 1024, 384, 1024, 1024, 2048
FLOPS = 2 * 2 * K * H * S + 2 * H * N * M

F32 = mybir.dt.float32
BF16 = mybir.dt.bfloat16
I32 = mybir.dt.int32
U32 = mybir.dt.uint32
U16 = mybir.dt.uint16
U8 = mybir.dt.uint8
FP8X4 = mybir.dt.float8_e4m3fn_x4
FP4X4 = mybir.dt.float4_e2m1fn_x4
ALU = mybir.AluOpType
ACT = mybir.ActivationFunctionType

P = 128
HALF = 512
CHUNK = 256
CHUNKS = M // CHUNK
TAIL = [(0, 256), (256, 256), (512, 256), (768, 128), (896, 128)]
PLANES = 8


def tile_list_lock_flight_adviser_kernel(
    tc, tab_words, tab_scales, offs, w1, b1, w2_words, w2_scales, wgs, offs2, wgt, offs3, lev, w3, out
):
    nc = tc.nc
    with ExitStack() as ctx:
        lists = ctx.enter_context(tc.tile_pool(name="lists", bufs=1))
        keep = ctx.enter_context(tc.tile_pool(name="keep", bufs=1))
        ring = ctx.enter_context(tc.tile_pool(name="ring", bufs=2))
        levs = ctx.enter_context(tc.tile_pool(name="levs", bufs=3))
        psum = ctx.enter_context(tc.psum_pool(name="psum", bufs=1))
        psum2 = ctx.enter_context(tc.psum_pool(name="psum2", bufs=2))

        list1 = lists.tile([P, S // 16], U16, name="list1")
        list2 = lists.tile([P, S // 16], U16, name="list2")
        list3 = lists.tile([P, M // 16], U16, name="list3")

        tab_plane = levs.tile([P, T], U8, name="tab_plane", tag="stage", align_bytes=64)
        nc.vector.memset(tab_plane[:].bitcast(I32), 0)
        w2_plane_raw = levs.tile([P, H], U8, name="w2_plane_raw", tag="stage", align_bytes=64)
        nc.gpsimd.memset(w2_plane_raw[:].bitcast(I32), 0)

        nc.sync.dma_start(list1[:], offs)
        nc.sync.dma_start(list2[:], offs2)
        nc.sync.dma_start(list3[:], offs3)
        bias = keep.tile([P, 2, 4], F32, name="bias")
        nc.sync.dma_start(bias[:], b1.rearrange("(b p i) -> p b i", b=2, i=4))
        w2_raw = keep.tile([P, 2 * H], U8, name="w2_raw", tag="put_weight", align_bytes=64)
        nc.sync.dma_start(w2_raw[:].bitcast(I32), w2_words[0].bitcast(I32))
        for q in range(4):
            nc.scalar.dma_start(
                tab_plane[32 * q : 32 * q + 4, :].bitcast(I32), tab_scales[0, 4 * q : 4 * q + 4, :].bitcast(I32)
            )
        for q in range(4):
            nc.gpsimd.dma_start(
                w2_plane_raw[32 * q : 32 * q + 4, :].bitcast(I32), w2_scales[0, 4 * q : 4 * q + 4, :].bitcast(I32)
            )

        w1_rows = w1.rearrange("(p j) c -> p j c", j=4)
        w1_codes, w1_planes = [], []

        def load_w1(b):
            raw = keep.tile([P, 4, HALF], F32, name="w1_raw", tag="raw")
            nc.sync.dma_start(raw[:], w1_rows[:, :, b * HALF : (b + 1) * HALF])
            return raw

        def quantise_w1(b, raw):
            grouped = levs.tile([P, 4 * HALF], BF16, name="w1_grouped", tag=("stage", "later")[b], align_bytes=64)
            nc.scalar.copy(
                grouped[:].rearrange("p (i q j) -> p q i j", i=4, j=4),
                raw[:].rearrange("p j (q i) -> p q i j", i=4),
            )
            codes = keep.tile([P, HALF], U32, name="w1_codes%d" % b, align_bytes=64)
            plane = keep.tile([P, HALF], U8, name="w1_plane%d" % b, align_bytes=64)
            nc.vector.quantize_mx(codes[:].bitcast(FP8X4), plane[:], grouped[:])
            w1_codes.append(codes)
            w1_planes.append(plane)

        w1_raw0 = load_w1(0)
        tab = keep.tile([P, T], I32, name="tab", tag="tab")
        nc.sync.dma_start(tab[:], tab_words[0].rearrange("p t i -> p (t i)").bitcast(I32))

        pages = []
        for k in range(2):
            page = keep.tile([P, T2], F32, name="page%d" % k)
            nc.vector.memset(page[:], 0.0)
            pages.append(page)
        ident = keep.tile([P, P], F32, name="ident")
        make_identity(nc, ident[:])
        ident_bf16 = keep.tile([P, P], BF16, name="ident_bf16")
        make_identity(nc, ident_bf16[:])

        w2_codes = keep.tile([P, 2 * H], U8, name="w2_codes", align_bytes=64)
        nc.vector.tensor_copy(
            w2_codes[:].bitcast(U16).rearrange("p (b i q) -> p b i q", b=2, i=4),
            w2_raw[:].bitcast(U16).rearrange("p (b q i) -> p b i q", b=2, i=4),
        )
        put_weight = keep.tile([P, S], F32, name="put_weight", tag="put_weight", align_bytes=64)
        nc.sync.dma_start(put_weight[:], wgs)
        v_plane = keep.tile([P, S], U8, name="v_plane", align_bytes=64)
        nc.vector.tensor_copy(v_plane[:], tab_plane[:].indirect(list1[:]))
        w2_plane = keep.tile([P, H], U8, name="w2_plane", align_bytes=64)
        nc.vector.tensor_copy(
            w2_plane[:].rearrange("p (b i q) -> p b i q", b=2, i=4),
            w2_plane_raw[:].rearrange("p (b q i) -> p b i q", b=2, i=4),
        )
        quantise_w1(0, w1_raw0)

        v_codes = []
        for a in range(2):
            codes = keep.tile([P, HALF], U32, name="v_codes%d" % a, align_bytes=64)
            nc.vector.tensor_copy(codes[:], tab[:].bitcast(U32).indirect(list1[:, 32 * a : 32 * a + 32]))
            v_codes.append(codes)

        read_weight = keep.tile([P, M], F32, name="read_weight", tag="tab")
        nc.sync.dma_start(read_weight[:], wgt)
        minus_read_weight = keep.tile([P, M], F32, name="minus_read_weight")
        nc.scalar.mul(minus_read_weight[:], read_weight[:], -1.0)

        lev_rows = lev.rearrange("(b p i) m -> b i p m", b=2, i=4)

        def load_lev(n):
            rows = levs.tile([P, M], F32, name="lev_rows", tag="stage", align_bytes=64)
            nc.sync.dma_start(rows[:], lev_rows[n // 4, n % 4])
            return rows

        w3_rows = w3.rearrange("(b p j) n -> b p j n", b=2, j=4)
        w3_codes, w3_planes = [], []

        def quantise_w3(b):
            raw = keep.tile([P, 4, N], F32, name="w3_raw", tag="raw")
            nc.sync.dma_start(raw[:], w3_rows[b])
            grouped = keep.tile([P, 4 * N], BF16, name="w3_grouped%d" % b, align_bytes=64)
            nc.scalar.copy(
                grouped[:].rearrange("p (c i j) -> p c j i", i=4, j=4),
                raw[:].rearrange("p j (c i) -> p c j i", i=4),
            )
            codes = keep.tile([P, N], U32, name="w3_codes%d" % b, align_bytes=64)
            plane = keep.tile([P, N], U8, name="w3_plane%d" % b, align_bytes=64)
            nc.vector.quantize_mx(codes[:].bitcast(FP8X4), plane[:], grouped[:])
            w3_codes.append(codes)
            w3_planes.append(plane)

        def tighter_score(n):
            b, i = divmod(n, 4)
            h = ring.tile([P, S], F32, name="h")
            room = ring.tile([P, S], F32, name="room")
            fills = []
            for a in range(2):
                cols = slice(a * HALF, (a + 1) * HALF)
                room_ps = psum.tile([P, HALF], F32, name="room_ps", tag="room%d" % a)
                nc.tensor.matmul_mx(
                    room_ps[:],
                    lhsT=w2_codes[:, 2 * P * n : 2 * P * (n + 1)].bitcast(FP4X4),
                    lhsT_scale=w2_plane[:, P * n : P * (n + 1)],
                    rhs=v_codes[a][:].bitcast(FP8X4),
                    rhs_scale=v_plane[:, cols],
                    start=True,
                    stop=True,
                )
                fill_ps = psum.tile([P, HALF], F32, name="fill_ps", tag="fill%d" % a)
                nc.tensor.matmul_mx(
                    fill_ps[:],
                    lhsT=w1_codes[b][:, P * i : P * (i + 1)].bitcast(FP8X4),
                    lhsT_scale=w1_planes[b][:, P * i : P * (i + 1)],
                    rhs=v_codes[a][:].bitcast(FP8X4),
                    rhs_scale=v_plane[:, cols],
                    start=True,
                    stop=True,
                )
                nc.scalar.copy(room[:, cols], room_ps[:])
                fills.append(fill_ps)
            for a in range(2):
                cols = slice(a * HALF, (a + 1) * HALF)
                nc.vector.scalar_tensor_tensor(
                    h[:, cols], fills[a][:], bias[:, b, i : i + 1], room[:, cols], ALU.add, ALU.min
                )
                if n == 0:
                    put(n, h, a * HALF, HALF)
            return h

        def put(n, h, first, count):
            cols = slice(first, first + count)
            nc.vector.tensor_tensor(
                pages[n % 2][:].indirect(list2[:, first // 16 : (first + count) // 16]),
                h[:, cols],
                put_weight[:, cols],
                ALU.mult,
            )

        def read(n, first, count):
            minus_x = ring.tile([P, count], F32, name="minus_x", tag="minus_x%d" % count, bufs=2 if count == M else 8)
            nc.vector.tensor_tensor(
                minus_x[:],
                pages[n % 2][:].indirect(list3[:, first // 16 : (first + count) // 16]),
                minus_read_weight[:, first : first + count],
                ALU.mult,
            )
            return minus_x

        spans = [[(0, HALF), (HALF, HALF)], TAIL]
        z_rows = [
            [keep.tile([P, 4 * M], BF16, name="z_rows0", align_bytes=64)],
            [
                keep.tile([P, 4 * count], BF16, name="z_rows1_%d" % c, align_bytes=64)
                for c, (first, count) in enumerate(TAIL)
            ],
        ]

        def z_slot(n, c):
            b, i = divmod(n, 4)
            first, count = spans[b][c]
            if b == 0:
                return z_rows[0][0][:].rearrange("p (m i) -> p m i", i=4)[:, first : first + count, i]
            return z_rows[1][c][:].rearrange("p (m i) -> p m i", i=4)[:, :, i]

        def turn(bank, rows, start, stop):
            blocks = rows.shape[1] // P
            for k in range(blocks):
                nc.tensor.matmul(
                    bank[:, k * P : (k + 1) * P],
                    rows[:, k * P : (k + 1) * P],
                    ident[:],
                    start=start and k == 0,
                    stop=stop and k == blocks - 1,
                    is_transpose=True,
                )

        def distance(n, lev_n, minus_x):
            for a in range(2):
                cols = slice(a * HALF, (a + 1) * HALF)
                bank = psum2.tile([P, HALF], F32, name="diff", tag="diff")
                turn(bank, lev_n[:, cols], True, False)
                turn(bank, minus_x[:, cols], False, True)
                turned = ring.tile([P, HALF], BF16, name="turned")
                nc.scalar.activation(turned[:], bank[:], ACT.Abs)
                back = psum2.tile([P, HALF], BF16, name="back", tag="back")
                for k in range(HALF // P):
                    block = slice(k * P, (k + 1) * P)
                    nc.tensor.transpose(back[:, block], turned[:, block], ident_bf16[:])
                for c, (first, count) in enumerate(spans[n // 4]):
                    if first // HALF == a:
                        nc.scalar.copy(z_slot(n, c), back[:, first - a * HALF : first - a * HALF + count])

        def quantise_z(rows, count, label):
            codes = keep.tile([P, count], U32, name="z_codes" + label, align_bytes=64)
            plane = keep.tile([P, count], U8, name="z_plane" + label, align_bytes=64)
            nc.vector.quantize_mx(codes[:].bitcast(FP8X4), plane[:], rows[:])
            return codes, plane

        out_rows = out.rearrange("(t p) m -> p t m", p=P)

        h_next = tighter_score(0)
        lev_tiles = [load_lev(0)]
        w1_raw1 = load_w1(1)
        lev_tiles.append(load_lev(1))
        for n in range(PLANES - 1):
            if n > 0:
                put(n, h_next, 0, S)
            h_next = tighter_score(n + 1)
            minus_x = read(n, 0, M)
            if n + 2 < PLANES:
                lev_tiles.append(load_lev(n + 2))
            distance(n, lev_tiles[n], minus_x)
            if n == 0:
                quantise_w1(1, w1_raw1)
            if n in (1, 2):
                quantise_w3(n - 1)
            if n == 5:
                z0_codes, z0_plane = quantise_z(z_rows[0][0], M, "0")

        last = PLANES - 1
        put(last, h_next, 0, S)

        def distance_last(c, minus_x):
            first, count = TAIL[c]
            difference = keep.tile([P, count], F32, name="difference_last%d" % c)
            nc.vector.tensor_tensor(difference[:], minus_x[:], lev_tiles[last][:, first : first + count], ALU.add)
            nc.scalar.activation(z_slot(last, c), difference[:], ACT.Abs)

        def multiply(c, b, accs, codes, plane):
            per_bank = accs[0].shape[1]
            for t in range(N // P):
                place = t % per_bank
                width = accs[t // per_bank].shape[1]
                nc.tensor.matmul_mx(
                    accs[t // per_bank][:, place, :],
                    lhsT=w3_codes[b][:, t * P : (t + 1) * P].bitcast(FP8X4),
                    lhsT_scale=w3_planes[b][:, t * P : (t + 1) * P],
                    rhs=codes.bitcast(FP8X4),
                    rhs_scale=plane,
                    start=(b == 0 and place == 0),
                    stop=(b == 1 and place == width - 1),
                )

        def open_sums(c, pool, tags):
            first, count = TAIL[c]
            widths = [2, 1] if len(tags) == 2 else [3]
            accs = [pool.tile([P, w, count], F32, name="acc", tag=tag) for w, tag in zip(widths, tags)]
            multiply(c, 0, accs, z0_codes[:, first : first + count], z0_plane[:, first : first + count])
            return accs

        def close_sums(c, accs, z1, copies):
            first, count = TAIL[c]
            multiply(c, 1, accs, z1[0][:], z1[1][:])
            result = ring.tile([P, N // P, count], F32, name="result", bufs=5)
            t = 0
            for acc, copy in zip(accs, copies):
                copy(result[:, t : t + acc.shape[1], :], acc[:])
                t = t + acc.shape[1]
            nc.sync.dma_start(out_rows[:, :, first : first + count], result[:])

        act, dve = nc.scalar.copy, nc.vector.tensor_copy
        places = [
            (psum, ["fill0", "fill1"]),
            (psum, ["room0", "room1"]),
            (psum2, ["diff", "diff"]),
            (psum2, ["back"]),
            (psum2, ["back"]),
        ]
        copies = [[dve, dve], [act, dve], [act, dve], [act], [dve]]
        accs = [open_sums(c, *places[c]) for c in range(len(TAIL))]
        xs = [read(last, *TAIL[0])]
        zs = []
        for c in range(len(TAIL)):
            if c + 1 < len(TAIL):
                xs.append(read(last, *TAIL[c + 1]))
            distance_last(c, xs[c])
            if c >= 2:
                zs.append(quantise_z(z_rows[1][c - 2], TAIL[c - 2][1], "1_%d" % (c - 2)))
        for c in range(len(TAIL)):
            if c + 3 < len(TAIL):
                zs.append(quantise_z(z_rows[1][c + 3], TAIL[c + 3][1], "1_%d" % (c + 3)))
            close_sums(c, accs[c], zs[c], copies[c])
